import numpy as np, ml_dtypes
CORES = [1,17,65,89,97,113]
N = 6
import mx_ref
NC = 128
BF = ml_dtypes.bfloat16
def setup_inputs(rng):
    def f(*shape):
        return mx_ref.flush((rng.standard_normal(shape, dtype=np.float32) * np.exp2(rng.integers(-2, 3, shape[:-1] + (1,)))).astype(BF))
    return {"w": f(N, 128, 512), "x": f(N, 128, N * 4 * NC)}
def setup_inputs_blocks(rng):
    d = setup_inputs(rng)
    for k in ("w", "x"): d[k] = mx_ref.spread(d[k], rng, 4)
    return d
def setup_inputs_wide(rng):
    d = setup_inputs(rng)
    for k in ("w", "x"): d[k] = mx_ref.flush((d[k].astype(np.float32) * np.exp2(rng.integers(-8, 9, (N, 1, 1))).astype(np.float32)).astype(BF))
    return d
def setup_inputs_zeros(rng):
    d = setup_inputs(rng); v = d["x"].reshape(N, 128, -1, 4).copy()
    v[np.broadcast_to((rng.random((N, 1, v.shape[2], 1)) < 0.33), v.shape)] = 0
    d["x"] = v.reshape(d["x"].shape)
    return d
def reference(w, x):
    y = np.zeros((N, 128, N * NC), np.float32)
    for r in range(N):
        qw = mx_ref.quantize(w[r])
        for j in range(N):
            y[r][:, NC * j:NC * j + NC] = mx_ref.matmul(qw, mx_ref.quantize(x[j][:, 4 * NC * r:4 * NC * r + 4 * NC]))
    return {"y": y}

@@ -1,0 +1,185 @@
+from concourse.bass import DstId, RemoteDMATransfer
+from concourse.mybir import dt
+
+N = 6
+NC = 128
+BANK = 512
+SELF = 2
+FIRST = 8
+
+SCRATCH = {
+    "xs": ("sbuf", [128, N * 4 * NC], "bfloat16"),
+    "ws": ("sbuf", [128, 4 * NC], "bfloat16"),
+    "qx": ("sbuf", [128, N * NC], "float8_e4m3fn_x4"),
+    "sx": ("sbuf", [128, N * NC], "uint8"),
+    "qw": ("sbuf", [128, NC], "float8_e4m3fn_x4"),
+    "sw": ("sbuf", [128, NC], "uint8"),
+    "rq": ("sbuf", [128, N * NC], "float8_e4m3fn_x4"),
+    "rs": ("sbuf", [128, N * NC], "uint8"),
+    "ysb": ("sbuf", [128, N * NC], "float32"),
+    "ps": ("psum", [128, N * BANK], "float32"),
+}
+SEMAPHORES = (["ld%d" % k for k in range(N + 1)] + ["q%d" % k for k in range(N + 1)]
+              + ["a%d" % k for k in range(N)] + ["b%d" % k for k in range(N)]
+              + ["mm%d" % k for k in range(N)] + ["cp%d" % k for k in range(N)] + ["sent", "st0", "st1"])
+
+
+def _bits(mask):
+    return [1 << i for i in range(mask.bit_length()) if (mask >> i) & 1]
+
+
+def _deal(pool, n):
+    if n == 0:
+        return []
+    size = 1
+    while size * 2 * n <= len(pool):
+        size *= 2
+    sizes = [size] * n
+    left = len(pool) - size * n
+    for i in range(n):
+        if left >= sizes[i]:
+            left -= sizes[i]
+            sizes[i] *= 2
+    out, at = [], 0
+    for s in sizes:
+        out.append(pool[at:at + s])
+        at += s
+    return out
+
+
+def _plan(T, topo):
+    cores = list(T.cores)
+    calls, tiles, when, due = {}, {}, {}, {}
+    for j, c in enumerate(cores):
+        ring = [(j + d) % N for d in range(1, N)]
+        far = [r for r in ring if not topo.may_write(c, cores[r])]
+        near = [r for r in ring if topo.may_write(c, cores[r])]
+        free = [k for k in range(topo.CHIPS * topo.CORES_PER_CHIP)
+                if topo.chip(k) == topo.chip(c) and k != c and k not in cores]
+        via = []
+        if far:
+            port = [k for k in free if all(topo.may_write(k, cores[r]) for r in far)]
+            mine = [k for k in port if topo.die(k) == topo.die(c)]
+            other = [k for k in port if topo.die(k) != topo.die(c)]
+            port = [k for pair in zip(mine, other) for k in pair]
+            turn = j if len(far) == 1 else 0
+            via = [(r, port[(i + turn) % len(port)]) for i, r in enumerate(far)]
+        own, rest = near[:SELF], near[SELF:]
+        taken = [h for _, h in via]
+        spare = [k for k in free if topo.die(k) != topo.die(c) and k not in taken]
+        spare.sort(key=lambda k: sum(topo.may_write(k, d) for d in cores))
+        via += [(r, spare[i]) for i, r in enumerate(rest)]
+        tiles[j] = [r for r, _ in via] + own + [j]
+
+        off = _bits(topo.mask(c, cores[own[0]])) if own else []
+        on = [b for b in _bits(topo.mask(c, via[0][1])) if b not in off]
+        q = lambda rs: [("q%d" % r, 1) for r in rs]
+        got = {}
+        mine = []
+        r0, h0 = via[0]
+        got[(r0, "c")] = on[:FIRST]
+        mine.append((q([r0]), "c", [(r0, h0, r0, on[:FIRST], "a%d" % r0)]))
+        trs = []
+        for (r, h), e in zip(via[1:], _deal(on, len(via) - 1)):
+            got[(r, "c")] = e
+            trs.append((r, h, r, e, "a%d" % r))
+        for r, e in zip(own, _deal(off, len(own))):
+            trs.append((r, cores[r], j, e, "a%d" % j))
+        mine.append((q([r for r, _ in via[1:]] + own), "c", trs))
+        trs = []
+        for (r, h), e in zip(via, _deal(on, len(via))):
+            got[(r, "s")] = e
+            trs.append((r, h, r, e, "b%d" % r))
+        for r, e in zip(own, _deal(off, len(own))):
+            trs.append((r, cores[r], j, e, "a%d" % j))
+        mine.append(([], "s", trs))
+        calls[c] = mine
+        for i, r in enumerate(own):
+            when[(j, r)] = (1, 0, i)
+        for h in sorted(set(taken + [h for _, h in via])):
+            rs = [r for r, k in via if k == h]
+            prog = []
+            for n, r in enumerate(rs):
+                prog.append(([("a%d" % r, len(got[(r, "c")]))], "c",
+                             [(r, cores[r], j, _bits(topo.mask(h, cores[r])), "a%d" % j)]))
+                when[(j, r)] = (2, n, [x for x, _ in via].index(r))
+            prog.append(([("b%d" % r, len(got[(r, "s")])) for r in rs], "s",
+                         [(r, cores[r], j, e, "a%d" % j)
+                          for r, e in zip(rs, _deal(_bits(topo.mask(h, cores[rs[0]])), len(rs)))]))
+            calls[h] = prog
+    for c in calls:
+        for _, _, trs in calls[c]:
+            for _, d, _, e, s in trs:
+                due[(d, s)] = due.get((d, s), 0) + len(e)
+    return calls, tiles, when, due
+
+
+def _send(g, T, topo, prog, is_rank):
+    left = 0
+    for waits, kind, trs in prog:
+        for s, v in waits:
+            g.wait_ge(T.sem[s], v)
+        made = []
+        for a, d, b, e, s in trs:
+            if kind == "c":
+                src = (T.qx if is_rank else T.rq)[:, a * NC:(a + 1) * NC].bitcast(dt.uint8)
+                dst = T.rq[:, b * NC:(b + 1) * NC].bitcast(dt.uint8)
+            else:
+                src = (T.sx if is_rank else T.rs)[:, a * NC:(a + 1) * NC]
+                dst = T.rs[:, b * NC:(b + 1) * NC]
+            rid, pid, _ = topo.addr(d)
+            made.append((src, dst, rid, pid, sum(e), T.sem[s]))
+            left += len(e)
+        if len(made) == 1:
+            src, dst, rid, pid, m, s = made[0]
+            g.remote_dma(out_ap=dst, in_ap=src, remote_sem=s, local_sem=T.sem.sent, pid=pid, routing_id=rid,
+                         dma_engine_mask=m)
+        else:
+            g.remote_dma_fused([RemoteDMATransfer(dst_ids=[DstId(rid=rid, pnc=pid)], dma_engine_mask=m, remote_sem=s,
+                                                  src=src, dst=dst) for src, dst, rid, pid, m, s in made],
+                               local_sem=T.sem.sent)
+    g.wait_ge(T.sem.sent, left)
+
+
+def rank_program(g, core, T, topo):
+    calls, tiles, when, due = _plan(T, topo)
+    me = T.rank_of(core)
+    if me is None:
+        if core in calls:
+            _send(g, T, topo, calls[core], False)
+        return
+
+    local = [g.sync, g.scalar]
+    for i, r in enumerate(tiles[me]):
+        local[i % 2].dma_start(T.xs[:, r * 4 * NC:(r + 1) * 4 * NC], T.x[:, r * 4 * NC:(r + 1) * 4 * NC]).then_inc(T.sem["ld%d" % r], 16)
+    local[N % 2].dma_start(T.ws[:], T.w[:]).then_inc(T.sem["ld%d" % N], 16)
+    for r in tiles[me]:
+        g.vector.wait_ge(T.sem["ld%d" % r], 16)
+        g.vector.quantize_mx(T.qx[:, r * NC:(r + 1) * NC], T.sx[:, r * NC:(r + 1) * NC],
+                             T.xs[:, r * 4 * NC:(r + 1) * 4 * NC]).then_inc(T.sem["q%d" % r], 1)
+    g.vector.wait_ge(T.sem["ld%d" % N], 16)
+    g.vector.quantize_mx(T.qw[:], T.sw[:], T.ws[:]).then_inc(T.sem["q%d" % N], 1)
+
+    _send(g, T, topo, calls[core], True)
+
+    order = [me] + sorted([j for j in range(N) if j != me], key=lambda j: when[(j, me)])
+    g.tensor.wait_ge(T.sem["q%d" % N], 1)
+    stored = [0, 0]
+    for i, j in enumerate(order):
+        cols = slice(j * NC, (j + 1) * NC)
+        if j == me:
+            g.tensor.wait_ge(T.sem["q%d" % me], 1)
+            codes, plane = T.qx[:, cols], T.sx[:, cols]
+        else:
+            g.tensor.wait_ge(T.sem["a%d" % j], due[(core, "a%d" % j)])
+            codes, plane = T.rq[:, cols], T.rs[:, cols]
+        acc = T.ps[:, j * BANK:j * BANK + NC]
+        g.tensor.matmul_mx(acc, T.qw[:], T.sw[:], codes, plane, True, True).then_inc(T.sem["mm%d" % j], 1)
+        g.vector.wait_ge(T.sem["mm%d" % j], 1)
+        g.vector.tensor_copy(T.ysb[:, cols], acc).then_inc(T.sem["cp%d" % j], 1)
+        k = i % 2
+        local[k].wait_ge(T.sem["cp%d" % j], 1)
+        local[k].dma_start(T.y[:, cols], T.ysb[:, cols]).then_inc(T.sem["st%d" % k], 16)
+        stored[k] += 16
+    for k in range(2):
+        local[k].wait_ge(T.sem["st%d" % k], stored[k])

@@ -5,7 +5,6 @@ N = 6
 NC = 128
 BANK = 512
 SELF = 2
-FIRST = 8
 
 SCRATCH = {
     "xs": ("sbuf", [128, N * 4 * NC], "bfloat16"),
@@ -21,7 +20,7 @@ SCRATCH = {
 }
 SEMAPHORES = (["ld%d" % k for k in range(N + 1)] + ["q%d" % k for k in range(N + 1)]
               + ["a%d" % k for k in range(N)] + ["b%d" % k for k in range(N)]
-              + ["mm%d" % k for k in range(N)] + ["cp%d" % k for k in range(N)] + ["sent", "st0", "st1"])
+              + ["mm%d" % k for k in range(N)] + ["cp%d" % k for k in range(N)] + ["sent", "go", "st0", "st1"])
 
 
 def _bits(mask):
@@ -56,57 +55,46 @@ def _plan(T, topo):
         near = [r for r in ring if topo.may_write(c, cores[r])]
         free = [k for k in range(topo.CHIPS * topo.CORES_PER_CHIP)
                 if topo.chip(k) == topo.chip(c) and k != c and k not in cores]
-        via = []
-        if far:
-            port = [k for k in free if all(topo.may_write(k, cores[r]) for r in far)]
-            mine = [k for k in port if topo.die(k) == topo.die(c)]
-            other = [k for k in port if topo.die(k) != topo.die(c)]
-            port = [k for pair in zip(mine, other) for k in pair]
-            turn = j if len(far) == 1 else 0
-            via = [(r, port[(i + turn) % len(port)]) for i, r in enumerate(far)]
+        port = [k for k in free if all(topo.may_write(k, cores[r]) for r in far)]
+        mine = [k for k in port if topo.die(k) == topo.die(c)]
+        other = [k for k in port if topo.die(k) != topo.die(c)]
+        port = [k for pair in zip(mine, other) for k in pair]
+        turn = j if len(far) == 1 else 0
+        via = [(r, port[(i + turn) % len(port)]) for i, r in enumerate(far)]
         own, rest = near[:SELF], near[SELF:]
         taken = [h for _, h in via]
-        spare = [k for k in free if topo.die(k) != topo.die(c) and k not in taken]
+        spare = [k for k in free if topo.die(k) == topo.die(c) and k not in taken]
         spare.sort(key=lambda k: sum(topo.may_write(k, d) for d in cores))
         via += [(r, spare[i]) for i, r in enumerate(rest)]
         tiles[j] = [r for r, _ in via] + own + [j]
 
+        every = _bits(topo.mask(c, via[0][1]))
         off = _bits(topo.mask(c, cores[own[0]])) if own else []
-        on = [b for b in _bits(topo.mask(c, via[0][1])) if b not in off]
+        on = [b for b in every if b not in off]
+        one = on[:len(every) // 2]
+        two = [b for b in every if b not in one]
         q = lambda rs: [("q%d" % r, 1) for r in rs]
-        got = {}
-        mine = []
+        prog = {h: [] for _, h in via}
+
+        def hand(kind, r, h, e):
+            s = ("a%d" if kind == "c" else "b%d") % r
+            prog[h].append(([(s, len(e))], kind, [(r, cores[r], j, _bits(topo.mask(h, cores[r])), "a%d" % j)]))
+            return (r, h, r, e, s)
+
         r0, h0 = via[0]
-        got[(r0, "c")] = on[:FIRST]
-        mine.append((q([r0]), "c", [(r0, h0, r0, on[:FIRST], "a%d" % r0)]))
-        trs = []
-        for (r, h), e in zip(via[1:], _deal(on, len(via) - 1)):
-            got[(r, "c")] = e
-            trs.append((r, h, r, e, "a%d" % r))
-        for r, e in zip(own, _deal(off, len(own))):
-            trs.append((r, cores[r], j, e, "a%d" % j))
-        mine.append((q([r for r, _ in via[1:]] + own), "c", trs))
-        trs = []
-        for (r, h), e in zip(via, _deal(on, len(via))):
-            got[(r, "s")] = e
-            trs.append((r, h, r, e, "b%d" % r))
-        for r, e in zip(own, _deal(off, len(own))):
-            trs.append((r, cores[r], j, e, "a%d" % j))
-        mine.append(([], "s", trs))
+        h1 = via[1][1] if len(far) > 1 else h0
+        mine = [(q([r0]), "c", [hand("c", r0, h0, one)]), ([], "s", [hand("s", r0, h1, two)])]
+        for kind in "cs":
+            trs = [hand(kind, r, h, e) for (r, h), e in zip(via[1:], _deal(on, len(via) - 1))]
+            trs += [(r, cores[r], j, e, "a%d" % j) for r, e in zip(own, _deal(off, len(own)))]
+            mine.append((q([r for r, _ in via[1:]] + own) if kind == "c" else [], kind, trs))
         calls[c] = mine
+        calls.update(prog)
+        when[(j, r0)] = (0, 0)
         for i, r in enumerate(own):
-            when[(j, r)] = (1, 0, i)
-        for h in sorted(set(taken + [h for _, h in via])):
-            rs = [r for r, k in via if k == h]
-            prog = []
-            for n, r in enumerate(rs):
-                prog.append(([("a%d" % r, len(got[(r, "c")]))], "c",
-                             [(r, cores[r], j, _bits(topo.mask(h, cores[r])), "a%d" % j)]))
-                when[(j, r)] = (2, n, [x for x, _ in via].index(r))
-            prog.append(([("b%d" % r, len(got[(r, "s")])) for r in rs], "s",
-                         [(r, cores[r], j, e, "a%d" % j)
-                          for r, e in zip(rs, _deal(_bits(topo.mask(h, cores[rs[0]])), len(rs)))]))
-            calls[h] = prog
+            when[(j, r)] = (1, i)
+        for i, (r, h) in enumerate(via[1:]):
+            when[(j, r)] = (2 + [x for x, k in via[1:] if k == h].index(r), i)
     for c in calls:
         for _, _, trs in calls[c]:
             for _, d, _, e, s in trs:
@@ -138,6 +126,8 @@ def _send(g, T, topo, prog, is_rank):
             g.remote_dma_fused([RemoteDMATransfer(dst_ids=[DstId(rid=rid, pnc=pid)], dma_engine_mask=m, remote_sem=s,
                                                   src=src, dst=dst) for src, dst, rid, pid, m, s in made],
                                local_sem=T.sem.sent)
+    if is_rank:
+        g.sem_inc(T.sem.go, 1)
     g.wait_ge(T.sem.sent, left)
 
 
@@ -151,7 +141,10 @@ def rank_program(g, core, T, topo):
 
     local = [g.sync, g.scalar]
     for i, r in enumerate(tiles[me]):
+        if r == me:
+            local[i % 2].wait_ge(T.sem.go, 1)
         local[i % 2].dma_start(T.xs[:, r * 4 * NC:(r + 1) * 4 * NC], T.x[:, r * 4 * NC:(r + 1) * 4 * NC]).then_inc(T.sem["ld%d" % r], 16)
+    local[N % 2].wait_ge(T.sem.go, 1)
     local[N % 2].dma_start(T.ws[:], T.w[:]).then_inc(T.sem["ld%d" % N], 16)
     for r in tiles[me]:
         g.vector.wait_ge(T.sem["ld%d" % r], 16)

from concourse.bass import DstId, RemoteDMATransfer
from concourse.mybir import dt

N = 6
NC = 128
BANK = 512
SELF = 2

SCRATCH = {
    "xs": ("sbuf", [128, N * 4 * NC], "bfloat16"),
    "ws": ("sbuf", [128, 4 * NC], "bfloat16"),
    "qx": ("sbuf", [128, N * NC], "float8_e4m3fn_x4"),
    "sx": ("sbuf", [128, N * NC], "uint8"),
    "qw": ("sbuf", [128, NC], "float8_e4m3fn_x4"),
    "sw": ("sbuf", [128, NC], "uint8"),
    "rq": ("sbuf", [128, N * NC], "float8_e4m3fn_x4"),
    "rs": ("sbuf", [128, N * NC], "uint8"),
    "ysb": ("sbuf", [128, N * NC], "float32"),
    "ps": ("psum", [128, N * BANK], "float32"),
}
SEMAPHORES = (["ld%d" % k for k in range(N + 1)] + ["q%d" % k for k in range(N + 1)]
              + ["a%d" % k for k in range(N)] + ["b%d" % k for k in range(N)]
              + ["mm%d" % k for k in range(N)] + ["cp%d" % k for k in range(N)] + ["sent", "go", "st0", "st1"])


def _bits(mask):
    return [1 << i for i in range(mask.bit_length()) if (mask >> i) & 1]


def _deal(pool, n):
    if n == 0:
        return []
    size = 1
    while size * 2 * n <= len(pool):
        size *= 2
    sizes = [size] * n
    left = len(pool) - size * n
    for i in range(n):
        if left >= sizes[i]:
            left -= sizes[i]
            sizes[i] *= 2
    out, at = [], 0
    for s in sizes:
        out.append(pool[at:at + s])
        at += s
    return out


def _plan(T, topo):
    cores = list(T.cores)
    calls, tiles, when, due = {}, {}, {}, {}
    for j, c in enumerate(cores):
        ring = [(j + d) % N for d in range(1, N)]
        far = [r for r in ring if not topo.may_write(c, cores[r])]
        near = [r for r in ring if topo.may_write(c, cores[r])]
        free = [k for k in range(topo.CHIPS * topo.CORES_PER_CHIP)
                if topo.chip(k) == topo.chip(c) and k != c and k not in cores]
        port = [k for k in free if all(topo.may_write(k, cores[r]) for r in far)]
        mine = [k for k in port if topo.die(k) == topo.die(c)]
        other = [k for k in port if topo.die(k) != topo.die(c)]
        port = [k for pair in zip(mine, other) for k in pair]
        turn = j if len(far) == 1 else 0
        via = [(r, port[(i + turn) % len(port)]) for i, r in enumerate(far)]
        own, rest = near[:SELF], near[SELF:]
        taken = [h for _, h in via]
        spare = [k for k in free if topo.die(k) == topo.die(c) and k not in taken]
        spare.sort(key=lambda k: sum(topo.may_write(k, d) for d in cores))
        via += [(r, spare[i]) for i, r in enumerate(rest)]
        tiles[j] = [r for r, _ in via] + own + [j]

        every = _bits(topo.mask(c, via[0][1]))
        off = _bits(topo.mask(c, cores[own[0]])) if own else []
        on = [b for b in every if b not in off]
        one = on[:len(every) // 2]
        two = [b for b in every if b not in one]
        q = lambda rs: [("q%d" % r, 1) for r in rs]
        prog = {h: [] for _, h in via}

        def hand(kind, r, h, e):
            s = ("a%d" if kind == "c" else "b%d") % r
            prog[h].append(([(s, len(e))], kind, [(r, cores[r], j, _bits(topo.mask(h, cores[r])), "a%d" % j)]))
            return (r, h, r, e, s)

        r0, h0 = via[0]
        h1 = via[1][1] if len(far) > 1 else h0
        mine = [(q([r0]), "c", [hand("c", r0, h0, one)]), ([], "s", [hand("s", r0, h1, two)])]
        for kind in "cs":
            trs = [hand(kind, r, h, e) for (r, h), e in zip(via[1:], _deal(on, len(via) - 1))]
            trs += [(r, cores[r], j, e, "a%d" % j) for r, e in zip(own, _deal(off, len(own)))]
            mine.append((q([r for r, _ in via[1:]] + own) if kind == "c" else [], kind, trs))
        calls[c] = mine
        calls.update(prog)
        when[(j, r0)] = (0, 0)
        for i, r in enumerate(own):
            when[(j, r)] = (1, i)
        for i, (r, h) in enumerate(via[1:]):
            when[(j, r)] = (2 + [x for x, k in via[1:] if k == h].index(r), i)
    for c in calls:
        for _, _, trs in calls[c]:
            for _, d, _, e, s in trs:
                due[(d, s)] = due.get((d, s), 0) + len(e)
    return calls, tiles, when, due


def _send(g, T, topo, prog, is_rank):
    left = 0
    for waits, kind, trs in prog:
        for s, v in waits:
            g.wait_ge(T.sem[s], v)
        made = []
        for a, d, b, e, s in trs:
            if kind == "c":
                src = (T.qx if is_rank else T.rq)[:, a * NC:(a + 1) * NC].bitcast(dt.uint8)
                dst = T.rq[:, b * NC:(b + 1) * NC].bitcast(dt.uint8)
            else:
                src = (T.sx if is_rank else T.rs)[:, a * NC:(a + 1) * NC]
                dst = T.rs[:, b * NC:(b + 1) * NC]
            rid, pid, _ = topo.addr(d)
            made.append((src, dst, rid, pid, sum(e), T.sem[s]))
            left += len(e)
        if len(made) == 1:
            src, dst, rid, pid, m, s = made[0]
            g.remote_dma(out_ap=dst, in_ap=src, remote_sem=s, local_sem=T.sem.sent, pid=pid, routing_id=rid,
                         dma_engine_mask=m)
        else:
            g.remote_dma_fused([RemoteDMATransfer(dst_ids=[DstId(rid=rid, pnc=pid)], dma_engine_mask=m, remote_sem=s,
                                                  src=src, dst=dst) for src, dst, rid, pid, m, s in made],
                               local_sem=T.sem.sent)
    if is_rank:
        g.sem_inc(T.sem.go, 1)
    g.wait_ge(T.sem.sent, left)


def rank_program(g, core, T, topo):
    calls, tiles, when, due = _plan(T, topo)
    me = T.rank_of(core)
    if me is None:
        if core in calls:
            _send(g, T, topo, calls[core], False)
        return

    local = [g.sync, g.scalar]
    for i, r in enumerate(tiles[me]):
        if r == me:
            local[i % 2].wait_ge(T.sem.go, 1)
        local[i % 2].dma_start(T.xs[:, r * 4 * NC:(r + 1) * 4 * NC], T.x[:, r * 4 * NC:(r + 1) * 4 * NC]).then_inc(T.sem["ld%d" % r], 16)
    local[N % 2].wait_ge(T.sem.go, 1)
    local[N % 2].dma_start(T.ws[:], T.w[:]).then_inc(T.sem["ld%d" % N], 16)
    for r in tiles[me]:
        g.vector.wait_ge(T.sem["ld%d" % r], 16)
        g.vector.quantize_mx(T.qx[:, r * NC:(r + 1) * NC], T.sx[:, r * NC:(r + 1) * NC],
                             T.xs[:, r * 4 * NC:(r + 1) * 4 * NC]).then_inc(T.sem["q%d" % r], 1)
    g.vector.wait_ge(T.sem["ld%d" % N], 16)
    g.vector.quantize_mx(T.qw[:], T.sw[:], T.ws[:]).then_inc(T.sem["q%d" % N], 1)

    _send(g, T, topo, calls[core], True)

    order = [me] + sorted([j for j in range(N) if j != me], key=lambda j: when[(j, me)])
    g.tensor.wait_ge(T.sem["q%d" % N], 1)
    stored = [0, 0]
    for i, j in enumerate(order):
        cols = slice(j * NC, (j + 1) * NC)
        if j == me:
            g.tensor.wait_ge(T.sem["q%d" % me], 1)
            codes, plane = T.qx[:, cols], T.sx[:, cols]
        else:
            g.tensor.wait_ge(T.sem["a%d" % j], due[(core, "a%d" % j)])
            codes, plane = T.rq[:, cols], T.rs[:, cols]
        acc = T.ps[:, j * BANK:j * BANK + NC]
        g.tensor.matmul_mx(acc, T.qw[:], T.sw[:], codes, plane, True, True).then_inc(T.sem["mm%d" % j], 1)
        g.vector.wait_ge(T.sem["mm%d" % j], 1)
        g.vector.tensor_copy(T.ysb[:, cols], acc).then_inc(T.sem["cp%d" % j], 1)
        k = i % 2
        local[k].wait_ge(T.sem["cp%d" % j], 1)
        local[k].dma_start(T.y[:, cols], T.ysb[:, cols]).then_inc(T.sem["st%d" % k], 16)
        stored[k] += 16
    for k in range(2):
        local[k].wait_ge(T.sem["st%d" % k], stored[k])
